import numpy as np
import ml_dtypes

BF16 = ml_dtypes.bfloat16


def bf(x):
    return np.asarray(x, np.float32).astype(BF16)


def f32(x):
    return np.asarray(x, np.float32)


def f64(x):
    return np.asarray(x).astype(np.float64)


def striped(idx):
    return np.tile(idx.reshape(-1, 16).T, (8, 1))


S, K, M, N, E, Q = 512, 128, 128, 512, 4, 128


def setup_inputs():
    return {"base": bf(np.random.standard_normal((M, S))), "x": bf(np.random.standard_normal((K, N))), "w": bf(np.random.standard_normal((E, K, M)) / np.sqrt(K)), "c": f32(0.2 + 0.8 * np.random.random_sample((1, S))), "offs": striped(np.random.permutation(S))}


def reference(base, x, w, c, offs):
    idx = offs[:16].T.reshape(-1)
    z = f64(base).copy()
    for e in range(E):
        z[:, idx[e * Q : (e + 1) * Q]] += f64(w)[e].T @ f64(x)[:, e * Q : (e + 1) * Q]
    return z * f64(c)

@@ -1,0 +1,53 @@
+import concourse.mybir as mybir
+from concourse.masks import make_identity
+
+BF16, F32, U16 = mybir.dt.bfloat16, mybir.dt.float32, mybir.dt.uint16
+
+P = 128
+TOKENS = 512
+EXPERTS = 4
+PIECE = 128
+PIECE_COLS = PIECE // 16
+
+FLOPS = 2 * P * P * EXPERTS * PIECE
+
+
+def tile_scatter_matmul_kernel(tc, base, x, w, c, offs, out):
+    nc = tc.nc
+    with (
+        tc.tile_pool(name="held", bufs=1) as held,
+        tc.psum_pool(name="psum", bufs=1) as psum,
+    ):
+        offsets = held.tile([P, EXPERTS * PIECE_COLS], U16, name="offsets")
+        nc.sync.dma_start(offsets[:], offs)
+
+        factors = held.tile([P, TOKENS], F32, name="factors")
+        nc.scalar.dma_start(factors[:], c.rearrange("o t -> (o t)").partition_broadcast(P))
+
+        base_tile = held.tile([P, TOKENS], BF16, name="base_tile")
+        nc.sync.dma_start(base_tile[:], base)
+
+        x_tile = held.tile([P, EXPERTS * PIECE], BF16, name="x_tile")
+        nc.sync.dma_start(x_tile[:], x)
+
+        w_tile = held.tile([P, EXPERTS, P], BF16, name="w_tile")
+        nc.scalar.dma_start(w_tile[:], w.rearrange("e k m -> k e m"))
+
+        identity = held.tile([P, P], BF16, name="identity")
+        make_identity(nc, identity[:])
+
+        window = psum.tile([P, TOKENS], F32, name="window")
+        nc.tensor.matmul(window[:], identity[:], base_tile[:], start=True, stop=False)
+
+        for e in range(EXPERTS):
+            nc.tensor.matmul(
+                window[:].indirect(offsets[:, e * PIECE_COLS : (e + 1) * PIECE_COLS]),
+                w_tile[:, e, :],
+                x_tile[:, e * PIECE : (e + 1) * PIECE],
+                start=False,
+                stop=(e == EXPERTS - 1),
+            )
+
+        result = held.tile([P, TOKENS], F32, name="result")
+        nc.vector.tensor_tensor(result[:], window[:], factors[:], mybir.AluOpType.mult)
+        nc.sync.dma_start(out, result[:])

@@ -8,6 +8,7 @@ TOKENS = 512
 EXPERTS = 4
 PIECE = 128
 PIECE_COLS = PIECE // 16
+HALF = TOKENS // 2
 
 FLOPS = 2 * P * P * EXPERTS * PIECE
 
@@ -21,9 +22,6 @@ def tile_scatter_matmul_kernel(tc, base, x, w, c, offs, out):
         offsets = held.tile([P, EXPERTS * PIECE_COLS], U16, name="offsets")
         nc.sync.dma_start(offsets[:], offs)
 
-        factors = held.tile([P, TOKENS], F32, name="factors")
-        nc.scalar.dma_start(factors[:], c.rearrange("o t -> (o t)").partition_broadcast(P))
-
         base_tile = held.tile([P, TOKENS], BF16, name="base_tile")
         nc.sync.dma_start(base_tile[:], base)
 
@@ -31,7 +29,12 @@ def tile_scatter_matmul_kernel(tc, base, x, w, c, offs, out):
         nc.sync.dma_start(x_tile[:], x)
 
         w_tile = held.tile([P, EXPERTS, P], BF16, name="w_tile")
-        nc.scalar.dma_start(w_tile[:], w.rearrange("e k m -> k e m"))
+        nc.sync.dma_start(w_tile[:], w.rearrange("e k m -> k e m"))
+
+        c_row = c.rearrange("o t -> (o t)")
+        factors = [held.tile([P, HALF], F32, name=f"factors{h}") for h in range(2)]
+        for h in range(2):
+            nc.sync.dma_start(factors[h][:], c_row[h * HALF : (h + 1) * HALF].partition_broadcast(P))
 
         identity = held.tile([P, P], BF16, name="identity")
         make_identity(nc, identity[:])
@@ -48,6 +51,9 @@ def tile_scatter_matmul_kernel(tc, base, x, w, c, offs, out):
                 stop=(e == EXPERTS - 1),
             )
 
-        result = held.tile([P, TOKENS], F32, name="result")
-        nc.vector.tensor_tensor(result[:], window[:], factors[:], mybir.AluOpType.mult)
-        nc.sync.dma_start(out, result[:])
+        for h in range(2):
+            columns = slice(h * HALF, (h + 1) * HALF)
+            result = held.tile([P, HALF], F32, name=f"result{h}")
+            nc.vector.tensor_tensor(result[:], window[:, columns], factors[h][:], mybir.AluOpType.mult)
+            store_queue = nc.sync if h == 0 else nc.scalar
+            store_queue.dma_start(out[:, columns], result[:])

@@ -19,17 +19,18 @@ def tile_scatter_matmul_kernel(tc, base, x, w, c, offs, out):
         tc.tile_pool(name="held", bufs=1) as held,
         tc.psum_pool(name="psum", bufs=1) as psum,
     ):
-        offsets = held.tile([P, EXPERTS * PIECE_COLS], U16, name="offsets")
-        nc.sync.dma_start(offsets[:], offs)
-
         base_tile = held.tile([P, TOKENS], BF16, name="base_tile")
         nc.sync.dma_start(base_tile[:], base)
+
+        offsets = held.tile([P, EXPERTS * PIECE_COLS], U16, name="offsets")
+        nc.sync.dma_start(offsets[:], offs)
 
         x_tile = held.tile([P, EXPERTS * PIECE], BF16, name="x_tile")
         nc.sync.dma_start(x_tile[:], x)
 
-        w_tile = held.tile([P, EXPERTS, P], BF16, name="w_tile")
-        nc.sync.dma_start(w_tile[:], w.rearrange("e k m -> k e m"))
+        w_tiles = [held.tile([P, P], BF16, name=f"w_tile{e}") for e in range(EXPERTS)]
+        for e in range(EXPERTS):
+            nc.sync.dma_start(w_tiles[e][:], w[e])
 
         c_row = c.rearrange("o t -> (o t)")
         factors = [held.tile([P, HALF], F32, name=f"factors{h}") for h in range(2)]
@@ -45,7 +46,7 @@ def tile_scatter_matmul_kernel(tc, base, x, w, c, offs, out):
         for e in range(EXPERTS):
             nc.tensor.matmul(
                 window[:].indirect(offsets[:, e * PIECE_COLS : (e + 1) * PIECE_COLS]),
-                w_tile[:, e, :],
+                w_tiles[e][:],
                 x_tile[:, e * PIECE : (e + 1) * PIECE],
                 start=False,
                 stop=(e == EXPERTS - 1),

@@ -8,6 +8,7 @@ TOKENS = 512
 EXPERTS = 4
 PIECE = 128
 PIECE_COLS = PIECE // 16
+BLOCKS = TOKENS // P
 HALF = TOKENS // 2
 
 FLOPS = 2 * P * P * EXPERTS * PIECE
@@ -22,6 +23,9 @@ def tile_scatter_matmul_kernel(tc, base, x, w, c, offs, out):
         base_tile = held.tile([P, TOKENS], BF16, name="base_tile")
         nc.sync.dma_start(base_tile[:], base)
 
+        c_cols = held.tile([P, BLOCKS], F32, name="c_cols")
+        nc.sync.dma_start(c_cols[:], c.rearrange("o (a p) -> p (o a)", p=P))
+
         offsets = held.tile([P, EXPERTS * PIECE_COLS], U16, name="offsets")
         nc.sync.dma_start(offsets[:], offs)
 
@@ -32,16 +36,23 @@ def tile_scatter_matmul_kernel(tc, base, x, w, c, offs, out):
         for e in range(EXPERTS):
             nc.sync.dma_start(w_tiles[e][:], w[e])
 
-        c_row = c.rearrange("o t -> (o t)")
-        factors = [held.tile([P, HALF], F32, name=f"factors{h}") for h in range(2)]
-        for h in range(2):
-            nc.sync.dma_start(factors[h][:], c_row[h * HALF : (h + 1) * HALF].partition_broadcast(P))
-
+        identity_f32 = held.tile([P, P], F32, name="identity_f32")
+        make_identity(nc, identity_f32[:])
         identity = held.tile([P, P], BF16, name="identity")
-        make_identity(nc, identity[:])
+        nc.vector.tensor_copy(identity[:], identity_f32[:])
 
         window = psum.tile([P, TOKENS], F32, name="window")
         nc.tensor.matmul(window[:], identity[:], base_tile[:], start=True, stop=False)
+
+        spread = psum.tile([P, TOKENS], F32, name="spread")
+        for a in range(BLOCKS):
+            nc.tensor.transpose(
+                spread[:, a * P : (a + 1) * P],
+                c_cols[:, a : a + 1].to_broadcast([P, P]),
+                identity_f32[:],
+            )
+        factors = held.tile([P, TOKENS], F32, name="factors")
+        nc.vector.tensor_copy(factors[:], spread[:])
 
         for e in range(EXPERTS):
             nc.tensor.matmul(
@@ -55,6 +66,6 @@ def tile_scatter_matmul_kernel(tc, base, x, w, c, offs, out):
         for h in range(2):
             columns = slice(h * HALF, (h + 1) * HALF)
             result = held.tile([P, HALF], F32, name=f"result{h}")
-            nc.vector.tensor_tensor(result[:], window[:, columns], factors[h][:], mybir.AluOpType.mult)
+            nc.vector.tensor_tensor(result[:], window[:, columns], factors[:, columns], mybir.AluOpType.mult)
             store_queue = nc.sync if h == 0 else nc.scalar
             store_queue.dma_start(out[:, columns], result[:])

@@ -9,6 +9,7 @@ EXPERTS = 4
 PIECE = 128
 PIECE_COLS = PIECE // 16
 BLOCKS = TOKENS // P
+WARM_UPS = 4
 HALF = TOKENS // 2
 
 FLOPS = 2 * P * P * EXPERTS * PIECE
@@ -35,6 +36,12 @@ def tile_scatter_matmul_kernel(tc, base, x, w, c, offs, out):
         w_tiles = [held.tile([P, P], BF16, name=f"w_tile{e}") for e in range(EXPERTS)]
         for e in range(EXPERTS):
             nc.sync.dma_start(w_tiles[e][:], w[e])
+
+        zeros = held.tile([P, TOKENS], BF16, name="zeros")
+        nc.vector.memset(zeros[:], 0.0)
+        unread = psum.tile([P, TOKENS], F32, name="unread")
+        for i in range(WARM_UPS):
+            nc.tensor.matmul(unread[:], zeros[:, :P], zeros[:], start=True, stop=True)
 
         identity_f32 = held.tile([P, P], F32, name="identity_f32")
         make_identity(nc, identity_f32[:])

@@ -25,7 +25,7 @@ def tile_scatter_matmul_kernel(tc, base, x, w, c, offs, out):
         nc.sync.dma_start(base_tile[:], base)
 
         c_cols = held.tile([P, BLOCKS], F32, name="c_cols")
-        nc.sync.dma_start(c_cols[:], c.rearrange("o (a p) -> p (o a)", p=P))
+        nc.sync.dma_start(c_cols[:], c.rearrange("o (p a) -> p (o a)", a=BLOCKS))
 
         offsets = held.tile([P, EXPERTS * PIECE_COLS], U16, name="offsets")
         nc.sync.dma_start(offsets[:], offs)
@@ -59,7 +59,10 @@ def tile_scatter_matmul_kernel(tc, base, x, w, c, offs, out):
                 identity_f32[:],
             )
         factors = held.tile([P, TOKENS], F32, name="factors")
-        nc.vector.tensor_copy(factors[:], spread[:])
+        nc.vector.tensor_copy(
+            factors[:].rearrange("p (j a) -> p j a", a=BLOCKS),
+            spread[:].rearrange("p (a j) -> p j a", a=BLOCKS),
+        )
 
         for e in range(EXPERTS):
             nc.tensor.matmul(

@@ -9,7 +9,7 @@ EXPERTS = 4
 PIECE = 128
 PIECE_COLS = PIECE // 16
 BLOCKS = TOKENS // P
-WARM_UPS = 4
+WARM_UPS = 3
 HALF = TOKENS // 2
 
 FLOPS = 2 * P * P * EXPERTS * PIECE

@@ -21,11 +21,11 @@ def tile_scatter_matmul_kernel(tc, base, x, w, c, offs, out):
         tc.tile_pool(name="held", bufs=1) as held,
         tc.psum_pool(name="psum", bufs=1) as psum,
     ):
-        base_tile = held.tile([P, TOKENS], BF16, name="base_tile")
-        nc.sync.dma_start(base_tile[:], base)
-
         c_cols = held.tile([P, BLOCKS], F32, name="c_cols")
         nc.sync.dma_start(c_cols[:], c.rearrange("o (p a) -> p (o a)", a=BLOCKS))
+
+        base_tile = held.tile([P, TOKENS], BF16, name="base_tile")
+        nc.sync.dma_start(base_tile[:], base)
 
         offsets = held.tile([P, EXPERTS * PIECE_COLS], U16, name="offsets")
         nc.sync.dma_start(offsets[:], offs)

@@ -77,5 +77,4 @@ def tile_scatter_matmul_kernel(tc, base, x, w, c, offs, out):
             columns = slice(h * HALF, (h + 1) * HALF)
             result = held.tile([P, HALF], F32, name=f"result{h}")
             nc.vector.tensor_tensor(result[:], window[:, columns], factors[:, columns], mybir.AluOpType.mult)
-            store_queue = nc.sync if h == 0 else nc.scalar
-            store_queue.dma_start(out[:, columns], result[:])
+            nc.sync.dma_start(out[:, columns], result[:])

@@ -33,9 +33,9 @@ def tile_scatter_matmul_kernel(tc, base, x, w, c, offs, out):
         x_tile = held.tile([P, EXPERTS * PIECE], BF16, name="x_tile")
         nc.sync.dma_start(x_tile[:], x)
 
-        w_tiles = [held.tile([P, P], BF16, name=f"w_tile{e}") for e in range(EXPERTS)]
-        for e in range(EXPERTS):
-            nc.sync.dma_start(w_tiles[e][:], w[e])
+        w_pairs = [held.tile([P, 2, P], BF16, name=f"w_pair{h}") for h in range(EXPERTS // 2)]
+        for h in range(EXPERTS // 2):
+            nc.sync.dma_start(w_pairs[h][:], w[2 * h : 2 * h + 2].rearrange("e k m -> k e m"))
 
         zeros = held.tile([P, TOKENS], BF16, name="zeros")
         nc.vector.memset(zeros[:], 0.0)
@@ -67,7 +67,7 @@ def tile_scatter_matmul_kernel(tc, base, x, w, c, offs, out):
         for e in range(EXPERTS):
             nc.tensor.matmul(
                 window[:].indirect(offsets[:, e * PIECE_COLS : (e + 1) * PIECE_COLS]),
-                w_tiles[e][:],
+                w_pairs[e // 2][:, e % 2, :],
                 x_tile[:, e * PIECE : (e + 1) * PIECE],
                 start=False,
                 stop=(e == EXPERTS - 1),

@@ -37,11 +37,13 @@ def tile_scatter_matmul_kernel(tc, base, x, w, c, offs, out):
         for h in range(EXPERTS // 2):
             nc.sync.dma_start(w_pairs[h][:], w[2 * h : 2 * h + 2].rearrange("e k m -> k e m"))
 
-        zeros = held.tile([P, TOKENS], BF16, name="zeros")
-        nc.vector.memset(zeros[:], 0.0)
+        zero = held.tile([P, 1], BF16, name="zero")
+        nc.vector.memset(zero[:], 0.0)
         unread = psum.tile([P, TOKENS], F32, name="unread")
         for i in range(WARM_UPS):
-            nc.tensor.matmul(unread[:], zeros[:, :P], zeros[:], start=True, stop=True)
+            nc.tensor.matmul(
+                unread[:], zero[:].to_broadcast([P, P]), zero[:].to_broadcast([P, TOKENS]), start=True, stop=True
+            )
 
         identity_f32 = held.tile([P, P], F32, name="identity_f32")
         make_identity(nc, identity_f32[:])

import concourse.mybir as mybir
from concourse.masks import make_identity

BF16, F32, U16 = mybir.dt.bfloat16, mybir.dt.float32, mybir.dt.uint16

P = 128
TOKENS = 512
EXPERTS = 4
PIECE = 128
PIECE_COLS = PIECE // 16
BLOCKS = TOKENS // P
WARM_UPS = 3
HALF = TOKENS // 2

FLOPS = 2 * P * P * EXPERTS * PIECE


def tile_scatter_matmul_kernel(tc, base, x, w, c, offs, out):
    nc = tc.nc
    with (
        tc.tile_pool(name="held", bufs=1) as held,
        tc.psum_pool(name="psum", bufs=1) as psum,
    ):
        c_cols = held.tile([P, BLOCKS], F32, name="c_cols")
        nc.sync.dma_start(c_cols[:], c.rearrange("o (p a) -> p (o a)", a=BLOCKS))

        base_tile = held.tile([P, TOKENS], BF16, name="base_tile")
        nc.sync.dma_start(base_tile[:], base)

        offsets = held.tile([P, EXPERTS * PIECE_COLS], U16, name="offsets")
        nc.sync.dma_start(offsets[:], offs)

        x_tile = held.tile([P, EXPERTS * PIECE], BF16, name="x_tile")
        nc.sync.dma_start(x_tile[:], x)

        w_pairs = [held.tile([P, 2, P], BF16, name=f"w_pair{h}") for h in range(EXPERTS // 2)]
        for h in range(EXPERTS // 2):
            nc.sync.dma_start(w_pairs[h][:], w[2 * h : 2 * h + 2].rearrange("e k m -> k e m"))

        zero = held.tile([P, 1], BF16, name="zero")
        nc.vector.memset(zero[:], 0.0)
        unread = psum.tile([P, TOKENS], F32, name="unread")
        for i in range(WARM_UPS):
            nc.tensor.matmul(
                unread[:], zero[:].to_broadcast([P, P]), zero[:].to_broadcast([P, TOKENS]), start=True, stop=True
            )

        identity_f32 = held.tile([P, P], F32, name="identity_f32")
        make_identity(nc, identity_f32[:])
        identity = held.tile([P, P], BF16, name="identity")
        nc.vector.tensor_copy(identity[:], identity_f32[:])

        window = psum.tile([P, TOKENS], F32, name="window")
        nc.tensor.matmul(window[:], identity[:], base_tile[:], start=True, stop=False)

        spread = psum.tile([P, TOKENS], F32, name="spread")
        for a in range(BLOCKS):
            nc.tensor.transpose(
                spread[:, a * P : (a + 1) * P],
                c_cols[:, a : a + 1].to_broadcast([P, P]),
                identity_f32[:],
            )
        factors = held.tile([P, TOKENS], F32, name="factors")
        nc.vector.tensor_copy(
            factors[:].rearrange("p (j a) -> p j a", a=BLOCKS),
            spread[:].rearrange("p (a j) -> p j a", a=BLOCKS),
        )

        for e in range(EXPERTS):
            nc.tensor.matmul(
                window[:].indirect(offsets[:, e * PIECE_COLS : (e + 1) * PIECE_COLS]),
                w_pairs[e // 2][:, e % 2, :],
                x_tile[:, e * PIECE : (e + 1) * PIECE],
                start=False,
                stop=(e == EXPERTS - 1),
            )

        for h in range(2):
            columns = slice(h * HALF, (h + 1) * HALF)
            result = held.tile([P, HALF], F32, name=f"result{h}")
            nc.vector.tensor_tensor(result[:], window[:, columns], factors[:, columns], mybir.AluOpType.mult)
            nc.sync.dma_start(out[:, columns], result[:])
